import numpy as np
import ml_dtypes


def mxq(x, axis, fmt="e4m3"):
    dtype, down = {"e4m3": (ml_dtypes.float8_e4m3fn, 7), "e5m2": (ml_dtypes.float8_e5m2, 14)}[fmt]
    v = np.moveaxis(np.asarray(x, np.float32).astype(ml_dtypes.bfloat16).astype(np.float64), axis, -1)
    blocks = v.reshape(v.shape[:-1] + (-1, 32))
    amax = np.abs(blocks).max(-1, keepdims=True)
    byte = np.maximum(np.where(amax > 0, np.frexp(amax)[1] - 1 + 127, 0) - down, 1)
    scale = np.exp2(byte - 127.0)
    codes = (blocks / scale).astype(np.float32).astype(dtype).astype(np.float64)
    return np.moveaxis((codes * scale).reshape(v.shape), -1, axis)


WIDE = False


def mx_kscale(k):
    if not WIDE:
        return np.ones(k)
    levels = np.array([10, -10, 5, -5, 0])
    if k % 512:
        return np.exp2(np.random.permutation(np.resize(levels, k // 32))).repeat(32)
    a = np.empty((k // 512, 16))
    for p in range(k // 512):
        a[p, :8] = np.random.permutation(np.resize(levels, 8))
        for g in range(8):
            far = levels[np.abs(levels - a[p, g]) >= 10]
            a[p, g + 8] = far[np.random.randint(len(far))]
    return np.exp2(a.ravel()).repeat(32)


def f64(x):
    return np.asarray(x).astype(np.float64)


def striped(idx):
    return np.tile(idx.reshape(-1, 16).T, (8, 1)).astype(np.uint16)


def unstriped(offs):
    return offs[:16].T.reshape(-1).astype(np.int64)


def pack_weight(w):
    k, n = w.shape
    w = f64(np.asarray(w, np.float32).astype(ml_dtypes.bfloat16)).reshape(k // 32, 32, n)
    amax = np.abs(w).max(1)
    byte = np.clip(np.where(amax > 0, np.frexp(amax)[1] - 1 + 127 - 7, 1), 1, 254)
    scaled = (w * np.exp2(127.0 - byte)[:, None, :]).reshape(k, n).astype(np.float32)
    words = np.ascontiguousarray(scaled.reshape(k // 512, 128, 4, n).transpose(0, 1, 3, 2)).astype(ml_dtypes.float8_e4m3fn).view(np.uint8)
    return words, np.ascontiguousarray(byte.astype(np.uint8).reshape(k // 512, 16, n))


def unpack_weight(words, scales):
    g, p, n, _ = words.shape
    vals = np.ascontiguousarray(words).view(ml_dtypes.float8_e4m3fn).astype(np.float64) * np.repeat(np.exp2(scales.astype(np.float64) - 127.0), 8, axis=1)[..., None]
    return vals.transpose(0, 1, 3, 2).reshape(g * 512, n)


def silu(v):
    return v / (1.0 + np.exp(-np.maximum(v, -700.0)))


K, T, S, H, N = 1024, 1024, 512, 512, 256


def setup_inputs():
    n = np.random.standard_normal
    s = mx_kscale(K)[:, None]
    u = mx_kscale(H)
    packed = pack_weight(n((K, T)) * s)
    return {
        "x_words": packed[0],
        "x_scales": packed[1],
        "w1": (n((K, H)) / np.sqrt(K) / s * u).astype(np.float32),
        "w2": (n((H, N)) / np.sqrt(H) / u[:, None]).astype(np.float32),
        "offs": striped(np.sort(np.random.permutation(T)[:S])),
    }


def reference(x_words, x_scales, w1, w2, offs):
    idx = unstriped(offs)
    xq = unpack_weight(x_words, x_scales)[:, idx]
    h = silu(mxq(f64(w1), 0, "e4m3").T @ xq)
    y = mxq(f64(w2), 0, "e4m3").T @ mxq(h, 0, "e4m3")
    return y

@@ -1,0 +1,179 @@
+from contextlib import ExitStack
+
+import concourse.mybir as mybir
+
+K, T, S, H, N = 1024, 1024, 512, 512, 256
+FLOPS = 2 * S * (K * H + H * N)
+
+F32 = mybir.dt.float32
+BF16 = mybir.dt.bfloat16
+I32 = mybir.dt.int32
+U32 = mybir.dt.uint32
+U16 = mybir.dt.uint16
+U8 = mybir.dt.uint8
+FP8X4 = mybir.dt.float8_e4m3fn_x4
+SILU = mybir.ActivationFunctionType.Silu
+
+P = 128
+PACK = 4
+PASSES = K // (P * PACK)
+HALF = H // 2
+QUADS = HALF // 16
+CHUNK = 128
+CHUNKS = S // CHUNK
+SCALAR_QUADS = [16, 6, 8, 6]
+
+
+def reach(c):
+    return CHUNK * (c + 1) + T - S
+
+
+def tile_picked_pick_mlp_silu_srt_p_kernel(tc, x_words, x_scales, w1, w2, offs, out):
+    nc = tc.nc
+    with ExitStack() as ctx:
+        keep = ctx.enter_context(tc.tile_pool(name="keep", bufs=1))
+        psum = ctx.enter_context(tc.psum_pool(name="psum", bufs=1))
+
+        offsets = keep.tile([P, S // 16], U16, name="offsets")
+        table_words = [keep.tile([P, T], I32, name=f"table_words{g}", align_bytes=64) for g in range(PASSES)]
+        table_scales = keep.tile([P, T], U8, name="table_scales", align_bytes=64)
+        w1_raw = [keep.tile([P, PACK, HALF], F32, name=f"w1_raw{i}", align_bytes=64) for i in range(2 * PASSES)]
+        w2_raw = keep.tile([P, PACK, N], F32, name="w2_raw", align_bytes=64)
+
+        def load_words(g, first, last):
+            words = x_words[g].rearrange("p n r -> p (n r)").bitcast(I32)
+            nc.sync.dma_start(out=table_words[g][:, first:last], in_=words[:, first:last])
+
+        def load_w1(g, half):
+            rows = w1[512 * g : 512 * (g + 1), HALF * half : HALF * (half + 1)]
+            nc.sync.dma_start(out=w1_raw[2 * g + half][:], in_=rows.rearrange("(p j) c -> p j c", j=PACK))
+
+        zero = keep.tile([P, 1], F32, name="zero")
+        no_bias = keep.tile([P, 1], F32, name="no_bias")
+        nc.vector.memset(table_scales[:].bitcast(I32), 0)
+        nc.vector.memset(zero[:], 0.0)
+        for q in range(4):
+            nc.scalar.dma_start(
+                out=table_scales[32 * q : 32 * q + 8, :].bitcast(I32),
+                in_=x_scales[:, 4 * q : 4 * q + 4, :].bitcast(I32),
+            )
+
+        nc.scalar.activation(out=no_bias[:], in_=zero[:], func=SILU)
+
+        load_words(0, 0, T)
+        nc.sync.dma_start(offsets[:], offs)
+        load_w1(0, 0)
+        load_w1(0, 1)
+        load_w1(1, 0)
+        load_w1(1, 1)
+        load_words(1, 0, reach(0))
+        load_words(1, reach(0), T)
+        w2_rows = w2.rearrange("(q t r) n -> t q r n", t=PACK, r=4)
+        for t in range(PACK):
+            nc.sync.dma_start(out=w2_raw[:, t, :], in_=w2_rows[t])
+
+        x_codes = [keep.tile([P, S], U32, name=f"x_codes{g}", align_bytes=64) for g in range(PASSES)]
+        x_planes = keep.tile([P, S], U8, name="x_planes", align_bytes=64)
+        w1_codes = [keep.tile([P, PACK, P], U32, name=f"w1_codes{g}", align_bytes=64) for g in range(PASSES)]
+        w1_planes = [keep.tile([P, PACK, P], U8, name=f"w1_planes{g}", align_bytes=64) for g in range(PASSES)]
+        w1_bf = [keep.tile([P, PACK, HALF], BF16, name=f"w1_bf{i}", align_bytes=64) for i in range(2 * PASSES)]
+        banks = [psum.tile([P, PACK, CHUNK], F32, name=f"hidden{c}") for c in range(CHUNKS)]
+
+        def gather_words(g, first, last):
+            nc.vector.tensor_copy(
+                x_codes[g][:, CHUNK * first : CHUNK * last],
+                table_words[g][:, : reach(last - 1)].bitcast(U32).indirect(offsets[:, 8 * first : 8 * last]),
+            )
+
+        def round_w1(piece):
+            src = w1_raw[piece][:].rearrange("p j (q t r) -> p q t j r", t=PACK, r=4)
+            dst = w1_bf[piece][:].rearrange("p t (q r j) -> p q t j r", r=4, j=PACK)
+            cut = SCALAR_QUADS[piece]
+            nc.scalar.copy(out=dst[:, :cut], in_=src[:, :cut])
+            if cut < QUADS:
+                nc.vector.tensor_copy(out=dst[:, cut:], in_=src[:, cut:])
+
+        def quantize_w1(piece):
+            g, half = divmod(piece, 2)
+            cols = slice(64 * half, 64 * (half + 1))
+            for t in range(PACK):
+                nc.vector.quantize_mx(
+                    out=w1_codes[g][:, t, cols].bitcast(FP8X4),
+                    scales=w1_planes[g][:, t, cols],
+                    in_=w1_bf[piece][:, t, :],
+                )
+
+        def first_product(g):
+            for c in range(CHUNKS):
+                cols = slice(CHUNK * c, CHUNK * (c + 1))
+                for t in range(PACK):
+                    nc.tensor.matmul_mx(
+                        out=banks[c][:, t, :],
+                        lhsT=w1_codes[g][:, t, :].bitcast(FP8X4),
+                        lhsT_scale=w1_planes[g][:, t, :],
+                        rhs=x_codes[g][:, cols].bitcast(FP8X4),
+                        rhs_scale=x_planes[4 * g : P, cols],
+                        start=(g == 0 and t == 0),
+                        stop=(g == PASSES - 1 and t == PACK - 1),
+                    )
+
+        gather_words(0, 0, CHUNKS)
+        round_w1(0)
+        nc.vector.tensor_copy(x_planes[:], table_scales[:].indirect(offsets[:]))
+        round_w1(1)
+        quantize_w1(0)
+        quantize_w1(1)
+        first_product(0)
+        round_w1(2)
+        quantize_w1(2)
+        round_w1(3)
+        quantize_w1(3)
+        for c in range(CHUNKS):
+            gather_words(1, c, c + 1)
+        first_product(1)
+
+        w2_bf = keep.tile([P, N, PACK], BF16, name="w2_bf", align_bytes=64)
+        w2_codes = keep.tile([P, N], U32, name="w2_codes", align_bytes=64)
+        w2_plane = keep.tile([P, N], U8, name="w2_plane", align_bytes=64)
+        h_bf = [keep.tile([P, CHUNK, PACK], BF16, name=f"h_bf{c}", align_bytes=64) for c in range(CHUNKS)]
+        h_codes = [keep.tile([P, CHUNK], U32, name=f"h_codes{c}", align_bytes=64) for c in range(CHUNKS)]
+        h_planes = [keep.tile([P, CHUNK], U8, name=f"h_plane{c}", align_bytes=64) for c in range(CHUNKS)]
+
+        def hidden(c):
+            nc.scalar.activation(out=h_bf[c][:], in_=banks[c][:].rearrange("p t n -> p n t"), func=SILU, bias=no_bias[:])
+            nc.vector.quantize_mx(
+                out=h_codes[c][:].bitcast(FP8X4), scales=h_planes[c][:], in_=h_bf[c][:].rearrange("p n t -> p (n t)")
+            )
+
+        hidden(0)
+        nc.vector.tensor_copy(
+            out=w2_bf[:].rearrange("p (a i) t -> p a t i", i=4),
+            in_=w2_raw[:].rearrange("p t (a i) -> p a t i", i=4),
+        )
+        hidden(1)
+        nc.vector.quantize_mx(
+            out=w2_codes[:].bitcast(FP8X4), scales=w2_plane[:], in_=w2_bf[:].rearrange("p n t -> p (n t)")
+        )
+        hidden(2)
+        hidden(3)
+
+        out_rows = out.rearrange("(u p) s -> p u s", p=P)
+        for c in range(CHUNKS):
+            y_bank = psum.tile([P, N // P, CHUNK], F32, name=f"result{c}")
+            for u in range(N // P):
+                rows = slice(P * u, P * (u + 1))
+                nc.tensor.matmul_mx(
+                    out=y_bank[:, u, :],
+                    lhsT=w2_codes[:, rows].bitcast(FP8X4),
+                    lhsT_scale=w2_plane[:, rows],
+                    rhs=h_codes[c][:].bitcast(FP8X4),
+                    rhs_scale=h_planes[c][:],
+                    start=True,
+                    stop=True,
+                )
+            y = keep.tile([P, N // P, CHUNK], F32, name=f"y{c}", align_bytes=64)
+            if c % 2 == 0:
+                nc.vector.tensor_copy(out=y[:], in_=y_bank[:])
+            else:
+                nc.scalar.copy(out=y[:], in_=y_bank[:])
+            nc.sync.dma_start(out=out_rows[:, :, CHUNK * c : CHUNK * (c + 1)], in_=y[:])

@@ -17,11 +17,8 @@ SILU = mybir.ActivationFunctionType.Silu
 P = 128
 PACK = 4
 PASSES = K // (P * PACK)
-HALF = H // 2
-QUADS = HALF // 16
 CHUNK = 128
 CHUNKS = S // CHUNK
-SCALAR_QUADS = [16, 6, 8, 6]
 
 
 def reach(c):
@@ -37,143 +34,147 @@ def tile_picked_pick_mlp_silu_srt_p_kernel(tc, x_words, x_scales, w1, w2, offs, 
         offsets = keep.tile([P, S // 16], U16, name="offsets")
         table_words = [keep.tile([P, T], I32, name=f"table_words{g}", align_bytes=64) for g in range(PASSES)]
         table_scales = keep.tile([P, T], U8, name="table_scales", align_bytes=64)
-        w1_raw = [keep.tile([P, PACK, HALF], F32, name=f"w1_raw{i}", align_bytes=64) for i in range(2 * PASSES)]
-        w2_raw = keep.tile([P, PACK, N], F32, name="w2_raw", align_bytes=64)
+        w1_first = keep.tile([P, PACK, H], F32, name="w1_first", align_bytes=64)
+        w1_second = [keep.tile([P, 2, H], F32, name=f"w1_second{i}", align_bytes=64) for i in range(2)]
+        w2_raw = keep.tile([P, PACK, N], F32, name="w2_raw", tag="w2_raw", align_bytes=64)
 
         def load_words(g, first, last):
             words = x_words[g].rearrange("p n r -> p (n r)").bitcast(I32)
             nc.sync.dma_start(out=table_words[g][:, first:last], in_=words[:, first:last])
 
-        def load_w1(g, half):
-            rows = w1[512 * g : 512 * (g + 1), HALF * half : HALF * (half + 1)]
-            nc.sync.dma_start(out=w1_raw[2 * g + half][:], in_=rows.rearrange("(p j) c -> p j c", j=PACK))
+        w1_rows = w1.rearrange("(g p j) c -> g p j c", p=P, j=PACK)
 
         zero = keep.tile([P, 1], F32, name="zero")
         no_bias = keep.tile([P, 1], F32, name="no_bias")
         nc.vector.memset(table_scales[:].bitcast(I32), 0)
         nc.vector.memset(zero[:], 0.0)
+        load_words(0, 0, T)
         for q in range(4):
-            nc.scalar.dma_start(
+            nc.sync.dma_start(
                 out=table_scales[32 * q : 32 * q + 8, :].bitcast(I32),
                 in_=x_scales[:, 4 * q : 4 * q + 4, :].bitcast(I32),
             )
 
         nc.scalar.activation(out=no_bias[:], in_=zero[:], func=SILU)
 
-        load_words(0, 0, T)
         nc.sync.dma_start(offsets[:], offs)
-        load_w1(0, 0)
-        load_w1(0, 1)
-        load_w1(1, 0)
-        load_w1(1, 1)
+        nc.sync.dma_start(out=w1_first[:], in_=w1_rows[0])
+        for i in range(2):
+            nc.sync.dma_start(out=w1_second[i][:], in_=w1_rows[1][:, 2 * i : 2 * i + 2, :])
         load_words(1, 0, reach(0))
         load_words(1, reach(0), T)
         w2_rows = w2.rearrange("(q t r) n -> t q r n", t=PACK, r=4)
         for t in range(PACK):
             nc.sync.dma_start(out=w2_raw[:, t, :], in_=w2_rows[t])
 
-        x_codes = [keep.tile([P, S], U32, name=f"x_codes{g}", align_bytes=64) for g in range(PASSES)]
+        x_first = keep.tile([P, S], U32, name="x_first", align_bytes=64)
+        x_head = keep.tile([P, CHUNK], U32, name="x_head", align_bytes=64)
         x_planes = keep.tile([P, S], U8, name="x_planes", align_bytes=64)
-        w1_codes = [keep.tile([P, PACK, P], U32, name=f"w1_codes{g}", align_bytes=64) for g in range(PASSES)]
-        w1_planes = [keep.tile([P, PACK, P], U8, name=f"w1_planes{g}", align_bytes=64) for g in range(PASSES)]
-        w1_bf = [keep.tile([P, PACK, HALF], BF16, name=f"w1_bf{i}", align_bytes=64) for i in range(2 * PASSES)]
-        banks = [psum.tile([P, PACK, CHUNK], F32, name=f"hidden{c}") for c in range(CHUNKS)]
+        w1_codes = [[keep.tile([P, P], U32, name=f"w1_codes{g}{t}", align_bytes=64) for t in range(PACK)] for g in range(PASSES)]
+        w1_planes = [[keep.tile([P, P], U8, name=f"w1_planes{g}{t}", align_bytes=64) for t in range(PACK)] for g in range(PASSES)]
+        w1_bf = [[keep.tile([P, H], BF16, name=f"w1_bf{g}{t}", tag=f"w1_bf{g}{t}", align_bytes=64) for t in range(PACK)] for g in range(PASSES)]
+        banks = [psum.tile([P, PACK, CHUNK], F32, name=f"hidden{c}", tag=f"hidden{c}") for c in range(CHUNKS)]
 
-        def gather_words(g, first, last):
+        def gather_words(dst, g, first, last):
             nc.vector.tensor_copy(
-                x_codes[g][:, CHUNK * first : CHUNK * last],
-                table_words[g][:, : reach(last - 1)].bitcast(U32).indirect(offsets[:, 8 * first : 8 * last]),
+                dst, table_words[g][:, : reach(last - 1)].bitcast(U32).indirect(offsets[:, 8 * first : 8 * last])
             )
 
-        def round_w1(piece):
-            src = w1_raw[piece][:].rearrange("p j (q t r) -> p q t j r", t=PACK, r=4)
-            dst = w1_bf[piece][:].rearrange("p t (q r j) -> p q t j r", r=4, j=PACK)
-            cut = SCALAR_QUADS[piece]
-            nc.scalar.copy(out=dst[:, :cut], in_=src[:, :cut])
-            if cut < QUADS:
-                nc.vector.tensor_copy(out=dst[:, cut:], in_=src[:, cut:])
-
-        def quantize_w1(piece):
-            g, half = divmod(piece, 2)
-            cols = slice(64 * half, 64 * (half + 1))
+        def round_w1(g, raw, slots, cut):
+            src = raw.rearrange("p j (q t r) -> p t q j r", t=PACK, r=4)
+            dst = [w1_bf[g][t][:].rearrange("p (q r j) -> p q j r", r=4, j=PACK)[:, :, slots] for t in range(PACK)]
             for t in range(PACK):
-                nc.vector.quantize_mx(
-                    out=w1_codes[g][:, t, cols].bitcast(FP8X4),
-                    scales=w1_planes[g][:, t, cols],
-                    in_=w1_bf[piece][:, t, :],
-                )
+                mid = min(max(cut - 32 * t, 0), 32)
+                if mid > 0:
+                    nc.vector.tensor_copy(out=dst[t][:, :mid], in_=src[:, t, :mid])
+                if mid < 32:
+                    nc.scalar.copy(out=dst[t][:, mid:], in_=src[:, t, mid:])
 
-        def first_product(g):
-            for c in range(CHUNKS):
-                cols = slice(CHUNK * c, CHUNK * (c + 1))
-                for t in range(PACK):
-                    nc.tensor.matmul_mx(
-                        out=banks[c][:, t, :],
-                        lhsT=w1_codes[g][:, t, :].bitcast(FP8X4),
-                        lhsT_scale=w1_planes[g][:, t, :],
-                        rhs=x_codes[g][:, cols].bitcast(FP8X4),
-                        rhs_scale=x_planes[4 * g : P, cols],
-                        start=(g == 0 and t == 0),
-                        stop=(g == PASSES - 1 and t == PACK - 1),
-                    )
+        def quantize_w1(g, t):
+            nc.vector.quantize_mx(out=w1_codes[g][t][:].bitcast(FP8X4), scales=w1_planes[g][t][:], in_=w1_bf[g][t][:])
 
-        gather_words(0, 0, CHUNKS)
-        round_w1(0)
+        def first_product(g, c, t, words):
+            cols = slice(CHUNK * c, CHUNK * (c + 1))
+            nc.tensor.matmul_mx(
+                out=banks[c][:, t, :],
+                lhsT=w1_codes[g][t][:].bitcast(FP8X4),
+                lhsT_scale=w1_planes[g][t][:],
+                rhs=words.bitcast(FP8X4),
+                rhs_scale=x_planes[4 * g : P, cols],
+                start=(g == 0 and t == 0),
+                stop=(g == PASSES - 1 and t == PACK - 1),
+            )
+
+        gather_words(x_first[:], 0, 0, CHUNKS)
         nc.vector.tensor_copy(x_planes[:], table_scales[:].indirect(offsets[:]))
-        round_w1(1)
-        quantize_w1(0)
-        quantize_w1(1)
-        first_product(0)
-        round_w1(2)
-        quantize_w1(2)
-        round_w1(3)
-        quantize_w1(3)
+        round_w1(0, w1_first[:], slice(0, PACK), 64)
+        for t in range(PACK):
+            quantize_w1(0, t)
+            for c in range(CHUNKS):
+                first_product(0, c, t, x_first[:, CHUNK * c : CHUNK * (c + 1)])
+        round_w1(1, w1_second[0][:], slice(0, 2), 64)
+        round_w1(1, w1_second[1][:], slice(2, 4), 64)
+        gather_words(x_head[:], 1, 0, 1)
+        for t in range(PACK):
+            quantize_w1(1, t)
+        x_rest = keep.tile([P, S - CHUNK], U32, name="x_rest", tag="w1_bf13", align_bytes=64)
+        second_words = [x_head[:]] + [x_rest[:, CHUNK * (c - 1) : CHUNK * c] for c in range(1, CHUNKS)]
+        for c in range(1, CHUNKS):
+            gather_words(second_words[c], 1, c, c + 1)
         for c in range(CHUNKS):
-            gather_words(1, c, c + 1)
-        first_product(1)
+            for t in range(PACK):
+                first_product(1, c, t, second_words[c])
 
         w2_bf = keep.tile([P, N, PACK], BF16, name="w2_bf", align_bytes=64)
         w2_codes = keep.tile([P, N], U32, name="w2_codes", align_bytes=64)
         w2_plane = keep.tile([P, N], U8, name="w2_plane", align_bytes=64)
         h_bf = [keep.tile([P, CHUNK, PACK], BF16, name=f"h_bf{c}", align_bytes=64) for c in range(CHUNKS)]
-        h_codes = [keep.tile([P, CHUNK], U32, name=f"h_codes{c}", align_bytes=64) for c in range(CHUNKS)]
+        h_words = keep.tile([P, CHUNKS, CHUNK], U32, name="h_words", tag="w2_raw", align_bytes=64)
         h_planes = [keep.tile([P, CHUNK], U8, name=f"h_plane{c}", align_bytes=64) for c in range(CHUNKS)]
 
         def hidden(c):
             nc.scalar.activation(out=h_bf[c][:], in_=banks[c][:].rearrange("p t n -> p n t"), func=SILU, bias=no_bias[:])
             nc.vector.quantize_mx(
-                out=h_codes[c][:].bitcast(FP8X4), scales=h_planes[c][:], in_=h_bf[c][:].rearrange("p n t -> p (n t)")
+                out=h_words[:, c, :].bitcast(FP8X4), scales=h_planes[c][:], in_=h_bf[c][:].rearrange("p n t -> p (n t)")
             )
 
-        hidden(0)
         nc.vector.tensor_copy(
             out=w2_bf[:].rearrange("p (a i) t -> p a t i", i=4),
             in_=w2_raw[:].rearrange("p t (a i) -> p a t i", i=4),
         )
-        hidden(1)
+        hidden(0)
         nc.vector.quantize_mx(
             out=w2_codes[:].bitcast(FP8X4), scales=w2_plane[:], in_=w2_bf[:].rearrange("p n t -> p (n t)")
         )
+        hidden(1)
         hidden(2)
         hidden(3)
 
         out_rows = out.rearrange("(u p) s -> p u s", p=P)
+
+        def second_product(dst, c, u):
+            rows = slice(P * u, P * (u + 1))
+            nc.tensor.matmul_mx(
+                out=dst,
+                lhsT=w2_codes[:, rows].bitcast(FP8X4),
+                lhsT_scale=w2_plane[:, rows],
+                rhs=h_words[:, c, :].bitcast(FP8X4),
+                rhs_scale=h_planes[c][:],
+                start=True,
+                stop=True,
+            )
+
+        copies = [nc.vector.tensor_copy, nc.scalar.copy]
         for c in range(CHUNKS):
-            y_bank = psum.tile([P, N // P, CHUNK], F32, name=f"result{c}")
-            for u in range(N // P):
-                rows = slice(P * u, P * (u + 1))
-                nc.tensor.matmul_mx(
-                    out=y_bank[:, u, :],
-                    lhsT=w2_codes[:, rows].bitcast(FP8X4),
-                    lhsT_scale=w2_plane[:, rows],
-                    rhs=h_codes[c][:].bitcast(FP8X4),
-                    rhs_scale=h_planes[c][:],
-                    start=True,
-                    stop=True,
-                )
             y = keep.tile([P, N // P, CHUNK], F32, name=f"y{c}", align_bytes=64)
-            if c % 2 == 0:
-                nc.vector.tensor_copy(out=y[:], in_=y_bank[:])
+            if c < CHUNKS - 1:
+                y_bank = psum.tile([P, N // P, CHUNK], F32, name=f"result{c}")
+                for u in range(N // P):
+                    second_product(y_bank[:, u, :], c, u)
+                copies[1 - c // 2](out=y[:], in_=y_bank[:])
             else:
-                nc.scalar.copy(out=y[:], in_=y_bank[:])
+                for u in range(N // P):
+                    y_half = psum.tile([P, CHUNK], F32, name=f"last{u}", tag=["last", "hidden0"][u])
+                    second_product(y_half[:], c, u)
+                    copies[u](out=y[:, u, :], in_=y_half[:])
             nc.sync.dma_start(out=out_rows[:, :, CHUNK * c : CHUNK * (c + 1)], in_=y[:])

from contextlib import ExitStack

import concourse.mybir as mybir

K, T, S, H, N = 1024, 1024, 512, 512, 256
FLOPS = 2 * S * (K * H + H * N)

F32 = mybir.dt.float32
BF16 = mybir.dt.bfloat16
I32 = mybir.dt.int32
U32 = mybir.dt.uint32
U16 = mybir.dt.uint16
U8 = mybir.dt.uint8
FP8X4 = mybir.dt.float8_e4m3fn_x4
SILU = mybir.ActivationFunctionType.Silu

P = 128
PACK = 4
PASSES = K // (P * PACK)
CHUNK = 128
CHUNKS = S // CHUNK


def reach(c):
    return CHUNK * (c + 1) + T - S


def tile_picked_pick_mlp_silu_srt_p_kernel(tc, x_words, x_scales, w1, w2, offs, out):
    nc = tc.nc
    with ExitStack() as ctx:
        keep = ctx.enter_context(tc.tile_pool(name="keep", bufs=1))
        psum = ctx.enter_context(tc.psum_pool(name="psum", bufs=1))

        offsets = keep.tile([P, S // 16], U16, name="offsets")
        table_words = [keep.tile([P, T], I32, name=f"table_words{g}", align_bytes=64) for g in range(PASSES)]
        table_scales = keep.tile([P, T], U8, name="table_scales", align_bytes=64)
        w1_first = keep.tile([P, PACK, H], F32, name="w1_first", align_bytes=64)
        w1_second = [keep.tile([P, 2, H], F32, name=f"w1_second{i}", align_bytes=64) for i in range(2)]
        w2_raw = keep.tile([P, PACK, N], F32, name="w2_raw", tag="w2_raw", align_bytes=64)

        def load_words(g, first, last):
            words = x_words[g].rearrange("p n r -> p (n r)").bitcast(I32)
            nc.sync.dma_start(out=table_words[g][:, first:last], in_=words[:, first:last])

        w1_rows = w1.rearrange("(g p j) c -> g p j c", p=P, j=PACK)

        zero = keep.tile([P, 1], F32, name="zero")
        no_bias = keep.tile([P, 1], F32, name="no_bias")
        nc.vector.memset(table_scales[:].bitcast(I32), 0)
        nc.vector.memset(zero[:], 0.0)
        load_words(0, 0, T)
        for q in range(4):
            nc.sync.dma_start(
                out=table_scales[32 * q : 32 * q + 8, :].bitcast(I32),
                in_=x_scales[:, 4 * q : 4 * q + 4, :].bitcast(I32),
            )

        nc.scalar.activation(out=no_bias[:], in_=zero[:], func=SILU)

        nc.sync.dma_start(offsets[:], offs)
        nc.sync.dma_start(out=w1_first[:], in_=w1_rows[0])
        for i in range(2):
            nc.sync.dma_start(out=w1_second[i][:], in_=w1_rows[1][:, 2 * i : 2 * i + 2, :])
        load_words(1, 0, reach(0))
        load_words(1, reach(0), T)
        w2_rows = w2.rearrange("(q t r) n -> t q r n", t=PACK, r=4)
        for t in range(PACK):
            nc.sync.dma_start(out=w2_raw[:, t, :], in_=w2_rows[t])

        x_first = keep.tile([P, S], U32, name="x_first", align_bytes=64)
        x_head = keep.tile([P, CHUNK], U32, name="x_head", align_bytes=64)
        x_planes = keep.tile([P, S], U8, name="x_planes", align_bytes=64)
        w1_codes = [[keep.tile([P, P], U32, name=f"w1_codes{g}{t}", align_bytes=64) for t in range(PACK)] for g in range(PASSES)]
        w1_planes = [[keep.tile([P, P], U8, name=f"w1_planes{g}{t}", align_bytes=64) for t in range(PACK)] for g in range(PASSES)]
        w1_bf = [[keep.tile([P, H], BF16, name=f"w1_bf{g}{t}", tag=f"w1_bf{g}{t}", align_bytes=64) for t in range(PACK)] for g in range(PASSES)]
        banks = [psum.tile([P, PACK, CHUNK], F32, name=f"hidden{c}", tag=f"hidden{c}") for c in range(CHUNKS)]

        def gather_words(dst, g, first, last):
            nc.vector.tensor_copy(
                dst, table_words[g][:, : reach(last - 1)].bitcast(U32).indirect(offsets[:, 8 * first : 8 * last])
            )

        def round_w1(g, raw, slots, cut):
            src = raw.rearrange("p j (q t r) -> p t q j r", t=PACK, r=4)
            dst = [w1_bf[g][t][:].rearrange("p (q r j) -> p q j r", r=4, j=PACK)[:, :, slots] for t in range(PACK)]
            for t in range(PACK):
                mid = min(max(cut - 32 * t, 0), 32)
                if mid > 0:
                    nc.vector.tensor_copy(out=dst[t][:, :mid], in_=src[:, t, :mid])
                if mid < 32:
                    nc.scalar.copy(out=dst[t][:, mid:], in_=src[:, t, mid:])

        def quantize_w1(g, t):
            nc.vector.quantize_mx(out=w1_codes[g][t][:].bitcast(FP8X4), scales=w1_planes[g][t][:], in_=w1_bf[g][t][:])

        def first_product(g, c, t, words):
            cols = slice(CHUNK * c, CHUNK * (c + 1))
            nc.tensor.matmul_mx(
                out=banks[c][:, t, :],
                lhsT=w1_codes[g][t][:].bitcast(FP8X4),
                lhsT_scale=w1_planes[g][t][:],
                rhs=words.bitcast(FP8X4),
                rhs_scale=x_planes[4 * g : P, cols],
                start=(g == 0 and t == 0),
                stop=(g == PASSES - 1 and t == PACK - 1),
            )

        gather_words(x_first[:], 0, 0, CHUNKS)
        nc.vector.tensor_copy(x_planes[:], table_scales[:].indirect(offsets[:]))
        round_w1(0, w1_first[:], slice(0, PACK), 64)
        for t in range(PACK):
            quantize_w1(0, t)
            for c in range(CHUNKS):
                first_product(0, c, t, x_first[:, CHUNK * c : CHUNK * (c + 1)])
        round_w1(1, w1_second[0][:], slice(0, 2), 64)
        round_w1(1, w1_second[1][:], slice(2, 4), 64)
        gather_words(x_head[:], 1, 0, 1)
        for t in range(PACK):
            quantize_w1(1, t)
        x_rest = keep.tile([P, S - CHUNK], U32, name="x_rest", tag="w1_bf13", align_bytes=64)
        second_words = [x_head[:]] + [x_rest[:, CHUNK * (c - 1) : CHUNK * c] for c in range(1, CHUNKS)]
        for c in range(1, CHUNKS):
            gather_words(second_words[c], 1, c, c + 1)
        for c in range(CHUNKS):
            for t in range(PACK):
                first_product(1, c, t, second_words[c])

        w2_bf = keep.tile([P, N, PACK], BF16, name="w2_bf", align_bytes=64)
        w2_codes = keep.tile([P, N], U32, name="w2_codes", align_bytes=64)
        w2_plane = keep.tile([P, N], U8, name="w2_plane", align_bytes=64)
        h_bf = [keep.tile([P, CHUNK, PACK], BF16, name=f"h_bf{c}", align_bytes=64) for c in range(CHUNKS)]
        h_words = keep.tile([P, CHUNKS, CHUNK], U32, name="h_words", tag="w2_raw", align_bytes=64)
        h_planes = [keep.tile([P, CHUNK], U8, name=f"h_plane{c}", align_bytes=64) for c in range(CHUNKS)]

        def hidden(c):
            nc.scalar.activation(out=h_bf[c][:], in_=banks[c][:].rearrange("p t n -> p n t"), func=SILU, bias=no_bias[:])
            nc.vector.quantize_mx(
                out=h_words[:, c, :].bitcast(FP8X4), scales=h_planes[c][:], in_=h_bf[c][:].rearrange("p n t -> p (n t)")
            )

        nc.vector.tensor_copy(
            out=w2_bf[:].rearrange("p (a i) t -> p a t i", i=4),
            in_=w2_raw[:].rearrange("p t (a i) -> p a t i", i=4),
        )
        hidden(0)
        nc.vector.quantize_mx(
            out=w2_codes[:].bitcast(FP8X4), scales=w2_plane[:], in_=w2_bf[:].rearrange("p n t -> p (n t)")
        )
        hidden(1)
        hidden(2)
        hidden(3)

        out_rows = out.rearrange("(u p) s -> p u s", p=P)

        def second_product(dst, c, u):
            rows = slice(P * u, P * (u + 1))
            nc.tensor.matmul_mx(
                out=dst,
                lhsT=w2_codes[:, rows].bitcast(FP8X4),
                lhsT_scale=w2_plane[:, rows],
                rhs=h_words[:, c, :].bitcast(FP8X4),
                rhs_scale=h_planes[c][:],
                start=True,
                stop=True,
            )

        copies = [nc.vector.tensor_copy, nc.scalar.copy]
        for c in range(CHUNKS):
            y = keep.tile([P, N // P, CHUNK], F32, name=f"y{c}", align_bytes=64)
            if c < CHUNKS - 1:
                y_bank = psum.tile([P, N // P, CHUNK], F32, name=f"result{c}")
                for u in range(N // P):
                    second_product(y_bank[:, u, :], c, u)
                copies[1 - c // 2](out=y[:], in_=y_bank[:])
            else:
                for u in range(N // P):
                    y_half = psum.tile([P, CHUNK], F32, name=f"last{u}", tag=["last", "hidden0"][u])
                    second_product(y_half[:], c, u)
                    copies[u](out=y[:, u, :], in_=y_half[:])
            nc.sync.dma_start(out=out_rows[:, :, CHUNK * c : CHUNK * (c + 1)], in_=y[:])
